import numpy as np
import ml_dtypes


def mxq(x, axis, fmt="e4m3"):
    dtype, down = {"e4m3": (ml_dtypes.float8_e4m3fn, 7), "e5m2": (ml_dtypes.float8_e5m2, 14)}[fmt]
    v = np.moveaxis(np.asarray(x, np.float32).astype(ml_dtypes.bfloat16).astype(np.float64), axis, -1)
    blocks = v.reshape(v.shape[:-1] + (-1, 32))
    amax = np.abs(blocks).max(-1, keepdims=True)
    byte = np.maximum(np.where(amax > 0, np.frexp(amax)[1] - 1 + 127, 0) - down, 1)
    scale = np.exp2(byte - 127.0)
    codes = (blocks / scale).astype(np.float32).astype(dtype).astype(np.float64)
    return np.moveaxis((codes * scale).reshape(v.shape), -1, axis)


WIDE = False


def mx_kscale(k):
    if not WIDE:
        return np.ones(k)
    levels = np.array([30, -30])
    if k % 512:
        return np.exp2(np.random.permutation(np.resize(levels, k // 32))).repeat(32)
    a = np.empty((k // 512, 16))
    for p in range(k // 512):
        a[p, :8] = np.random.permutation(np.resize(levels, 8))
        for g in range(8):
            far = levels[np.abs(levels - a[p, g]) >= 10]
            a[p, g + 8] = far[np.random.randint(len(far))]
    return np.exp2(a.ravel()).repeat(32)


def f64(x):
    return np.asarray(x).astype(np.float64)


def striped(idx):
    return np.tile(idx.reshape(-1, 16).T, (8, 1)).astype(np.uint16)


def unstriped(offs):
    return offs[:16].T.reshape(-1).astype(np.int64)


def d_relu(v):
    return (v > 0).astype(np.float64)


K, T, E, C, H, N = 768, 1024, 2, 512, 1024, 512


def by_expert(wq, xq):
    return np.concatenate([wq[e].T @ xq[:, e * C:(e + 1) * C] for e in range(E)], axis=1)


def setup_inputs():
    n = np.random.standard_normal
    s = mx_kscale(N)[:, None]
    u = mx_kscale(H)
    return {
        "dyT": (n((N, T)) * s).astype(np.float32),
        "a": n((H, E * C)).astype(np.float32),
        "w2": (n((E, N, H)) / np.sqrt(N) / s[None] * u[None, None, :]).astype(np.float32),
        "w1": (n((E, H, K)) / np.sqrt(H) / u[None, :, None]).astype(np.float32),
        "gate": np.tile(np.random.uniform(0.2, 1.0, E * C), (N, 1)).astype(np.float32),
        "offs": striped(np.random.permutation(T)[:E * C]),
    }


def reference(dyT, a, w2, w1, gate, offs):
    idx = unstriped(offs)
    gq = mxq(f64(gate) * f64(dyT)[:, idx], 0, "e5m2")
    dh = by_expert(mxq(f64(w2), 1, "e4m3"), gq)
    da = dh * d_relu(f64(a))
    dx = by_expert(mxq(f64(w1), 1, "e4m3"), mxq(da, 0, "e5m2"))
    out = np.zeros((K, T))
    out[:, idx] = dx
    return out

@@ -1,0 +1,210 @@
+from contextlib import ExitStack
+
+import concourse.mybir as mybir
+
+E, C, T = 2, 512, 1024
+K, H, N = 768, 1024, 512
+FLOPS = 2 * E * C * (N * H + H * K)
+BYTES = 4 * (N * T + H * E * C + E * N * H + E * H * K + E * C + K * T) + 2 * 128 * (E * C // 16)
+
+F32 = mybir.dt.float32
+BF16 = mybir.dt.bfloat16
+U32 = mybir.dt.uint32
+U16 = mybir.dt.uint16
+U8 = mybir.dt.uint8
+E4 = mybir.dt.float8_e4m3fn_x4
+E5 = mybir.dt.float8_e5m2_x4
+MULT = mybir.AluOpType.mult
+ADD = mybir.AluOpType.add
+IS_GT = mybir.AluOpType.is_gt
+
+P = 128
+HB = H // 512
+KT = K // P
+CHUNKS = ((0, 256), (256, 512))
+
+
+def tile_moe_bdx_mlp_relu_kernel(tc, dyT, a, w2, w1, gate, offs, out):
+    nc = tc.nc
+    with ExitStack() as ctx:
+        keep = ctx.enter_context(tc.tile_pool(name="keep", bufs=1))
+        ring = ctx.enter_context(tc.tile_pool(name="ring", bufs=2))
+        psum = ctx.enter_context(tc.psum_pool(name="psum", bufs=4))
+
+        def copy_on(eng, out_ap, in_ap):
+            if eng == "v":
+                nc.vector.tensor_copy(out=out_ap, in_=in_ap)
+            elif eng == "s":
+                nc.scalar.copy(out=out_ap, in_=in_ap)
+            else:
+                nc.gpsimd.tensor_scalar(out=out_ap, in0=in_ap, scalar1=1.0, scalar2=0.0, op0=MULT, op1=ADD)
+
+        def interleave(eng, dst, src):
+            if eng == "g":
+                copy_on(eng, dst.rearrange("p c t -> p c t"), src.rearrange("p t c -> p c t"))
+            else:
+                copy_on(eng, dst.rearrange("p (c i) t -> p c t i", i=4), src.rearrange("p t (c i) -> p c t i", i=4))
+
+        def quantize(src, width, fmt, name):
+            codes = keep.tile([P, width], U32, name=name + "_codes", align_bytes=64)
+            scales = keep.tile([P, width], U8, name=name + "_scales", align_bytes=64)
+            nc.vector.quantize_mx(out=codes[:].bitcast(fmt), scales=scales[:], in_=src)
+            return codes, scales
+
+        offs_t = keep.tile([P, E * C // 16], U16, name="offs_t")
+        nc.sync.dma_start(offs_t[:], offs)
+        dy_view = dyT.rearrange("(p t) j -> p t j", t=4)
+        dy = []
+        gates = []
+
+        def load_dy(t):
+            plane = keep.tile([P, T], F32, name="dy%d" % t)
+            nc.sync.dma_start(out=plane[:], in_=dy_view[:, t, :])
+            dy.append(plane)
+
+        def load_gate(e):
+            g = keep.tile([P, C], F32, name="gate%d" % e)
+            nc.sync.dma_start(out=g[:], in_=gate[0:P, e * C:(e + 1) * C])
+            gates.append(g)
+
+        def load_w2(e, b):
+            raw = ring.tile([P, 4, 512], F32, name="w2raw")
+            nc.sync.dma_start(out=raw[:], in_=w2[e, :, b * 512:(b + 1) * 512].rearrange("(p j) c -> p j c", j=4))
+            return raw
+
+        def load_a(e, b):
+            raw = ring.tile([P, 4, C], F32, name="araw")
+            nc.sync.dma_start(out=raw[:], in_=a[b * 512:(b + 1) * 512, e * C:(e + 1) * C].rearrange("(p t) j -> p t j", t=4))
+            return raw
+
+        def load_w1(e, b, q):
+            c0, cw = CHUNKS[q]
+            raw = ring.tile([P, 4, cw], F32, name="w1raw%d" % q)
+            nc.sync.dma_start(out=raw[:], in_=w1[e, b * 512:(b + 1) * 512, c0:c0 + cw].rearrange("(p j) c -> p j c", j=4))
+            return raw
+
+        def gather(e):
+            g4 = ring.tile([P, 4, C], F32, name="g4")
+            for t in range(4):
+                nc.vector.tensor_tensor(g4[:, t, :], dy[t][:].indirect(offs_t[:, e * (C // 16):(e + 1) * (C // 16)]), gates[e][:], MULT)
+            return g4
+
+        def make_g(e, g4, engs):
+            grouped = ring.tile([P, C, 4], BF16, name="ggrp", align_bytes=64)
+            w = C // len(engs)
+            for s, eng in enumerate(engs):
+                interleave(eng, grouped[:, s * w:(s + 1) * w, :], g4[:, :, s * w:(s + 1) * w])
+            return quantize(grouped[:].rearrange("p c t -> p (c t)"), C, E5, "g%d" % e)
+
+        def make_w2(e, b, raw, eng):
+            grouped = ring.tile([P, 2048], BF16, name="w2grp", align_bytes=64)
+            src = raw[:]
+            if eng == "g":
+                copy_on(eng, grouped[:].rearrange("p (t m j) -> p t m j", t=4, j=4), src.rearrange("p j (m t) -> p t m j", t=4))
+            else:
+                copy_on(eng, grouped[:].rearrange("p (t m j) -> p m j t", t=4, j=4), src.rearrange("p j (m t) -> p m j t", t=4))
+            return quantize(grouped[:], 512, E4, "w2_%d%d" % (e, b))
+
+        def make_w1(e, b, q, raw, eng):
+            cw = CHUNKS[q][1]
+            grouped = ring.tile([P, cw, 4], BF16, name="w1grp%d" % q, align_bytes=64)
+            interleave(eng, grouped[:], raw[:])
+            return quantize(grouped[:].rearrange("p c t -> p (c t)"), cw, E4, "w1_%d%d%d" % (e, b, q))
+
+        def dh_tile(w2q, gq, t):
+            bank = psum.tile([P, C], F32, name="dh")
+            cols = slice(t * P, (t + 1) * P)
+            nc.tensor.matmul_mx(out=bank[:], lhsT=w2q[0][:, cols].bitcast(E4), lhsT_scale=w2q[1][:, cols],
+                                rhs=gq[0][:].bitcast(E5), rhs_scale=gq[1][:], start=True, stop=True)
+            return bank
+
+        def da_vector(e, b, w2q, gq, raw, eng):
+            plain = ring.tile([P, 4, C], BF16, name="daplain", align_bytes=64)
+            for t in range(4):
+                bank = dh_tile(w2q, gq, t)
+                nc.vector.scalar_tensor_tensor(out=plain[:, t, :], in0=raw[:, t, :], scalar=0.0, in1=bank[:], op0=IS_GT, op1=MULT)
+            grouped = ring.tile([P, C, 4], BF16, name="dagrp", align_bytes=64)
+            for s in range(2):
+                interleave(eng, grouped[:, s * 256:(s + 1) * 256, :], plain[:, :, s * 256:(s + 1) * 256])
+            return quantize(grouped[:].rearrange("p c t -> p (c t)"), C, E5, "da_%d%d" % (e, b))
+
+        def make_mask(raw):
+            mask = ring.tile([P, C, 4], BF16, name="mask", align_bytes=64)
+            for s in range(2):
+                nc.gpsimd.tensor_scalar(out=mask[:, s * 256:(s + 1) * 256, :], in0=raw[:, :, s * 256:(s + 1) * 256].rearrange("p t c -> p c t"),
+                                        scalar1=0.0, scalar2=1.0, op0=IS_GT, op1=MULT)
+            return mask
+
+        def da_gpsimd(e, b, w2q, gq, mask):
+            plain = ring.tile([P, 4, C], BF16, name="daplain", align_bytes=64)
+            for t in range(4):
+                bank = dh_tile(w2q, gq, t)
+                nc.scalar.copy(out=plain[:, t, :], in_=bank[:])
+            grouped = ring.tile([P, C, 4], BF16, name="dagrp", align_bytes=64)
+            for s in range(2):
+                nc.gpsimd.tensor_tensor(grouped[:, s * 256:(s + 1) * 256, :], plain[:, :, s * 256:(s + 1) * 256].rearrange("p t c -> p c t"),
+                                        mask[:, s * 256:(s + 1) * 256, :], MULT)
+            return quantize(grouped[:].rearrange("p c t -> p (c t)"), C, E5, "da_%d%d" % (e, b))
+
+        windows = []
+        for kt in range(KT):
+            window = keep.tile([P, T], F32, name="window%d" % kt)
+            windows.append(window)
+
+        def dx_tile(kt, w1q, daq):
+            q = 0 if kt < 2 else 1
+            c0 = kt * P - CHUNKS[q][0]
+            cols = slice(c0, c0 + P)
+            bank = psum.tile([P, C], F32, name="dx")
+            for b in range(HB):
+                codes, scales = w1q[b, q]
+                nc.tensor.matmul_mx(out=bank[:], lhsT=codes[:, cols].bitcast(E4), lhsT_scale=scales[:, cols],
+                                    rhs=daq[b][0][:].bitcast(E5), rhs_scale=daq[b][1][:], start=(b == 0), stop=(b == HB - 1))
+            staged = ring.tile([P, C], F32, name="staged", bufs=6)
+            nc.scalar.copy(out=staged[:], in_=bank[:])
+            return staged
+
+        def scatter(e, kt, staged):
+            nc.vector.tensor_copy(out=windows[kt][:].indirect(offs_t[:, e * (C // 16):(e + 1) * (C // 16)]), in_=staged[:])
+
+        load_dy(0)
+        load_gate(0)
+        for t in range(1, 4):
+            load_dy(t)
+        w2raw = [load_w2(0, b) for b in range(HB)]
+        load_gate(1)
+        araw = [load_a(0, b) for b in range(HB)]
+        w1raw = {}
+        for q in range(2):
+            for b in range(HB):
+                w1raw[b, q] = load_w1(0, b, q)
+
+        g4 = gather(0)
+        gq = make_g(0, g4, "vs")
+        w2q = [make_w2(0, 0, w2raw[0], "v"), make_w2(0, 1, w2raw[1], "s")]
+        daq = [da_vector(0, b, w2q[b], gq, araw[b], "s") for b in range(HB)]
+        w1q = {}
+        for q, engs in ((0, "ss"), (1, "ss")):
+            for b in range(HB):
+                w1q[b, q] = make_w1(0, b, q, w1raw[b, q], engs[b])
+        staged0 = [dx_tile(kt, w1q, daq) for kt in range(KT)]
+
+        g4 = gather(1)
+        gq = make_g(1, g4, "s")
+        w2raw = [load_w2(1, b) for b in range(HB)]
+        araw = [load_a(1, b) for b in range(HB)]
+        for q in range(2):
+            for b in range(HB):
+                w1raw[b, q] = load_w1(1, b, q)
+        w2q = [make_w2(1, 0, w2raw[0], "s"), make_w2(1, 1, w2raw[1], "s")]
+        daq = [da_vector(1, b, w2q[b], gq, araw[b], "s") for b in range(HB)]
+        w1q = {}
+        for q, engs in ((0, "ss"), (1, "gg")):
+            for b in range(HB):
+                w1q[b, q] = make_w1(1, b, q, w1raw[b, q], engs[b])
+        for kt in range(KT):
+            scatter(0, kt, staged0[kt])
+        for kt in range(KT):
+            staged = dx_tile(kt, w1q, daq)
+            scatter(1, kt, staged)
+            nc.sync.dma_start(out=out[kt * P:(kt + 1) * P, :], in_=windows[kt][:])

@@ -17,6 +17,7 @@ E5 = mybir.dt.float8_e5m2_x4
 MULT = mybir.AluOpType.mult
 ADD = mybir.AluOpType.add
 IS_GT = mybir.AluOpType.is_gt
+ACT = mybir.ActivationFunctionType
 
 P = 128
 HB = H // 512
@@ -77,11 +78,14 @@ def tile_moe_bdx_mlp_relu_kernel(tc, dyT, a, w2, w1, gate, offs, out):
             nc.sync.dma_start(out=raw[:], in_=a[b * 512:(b + 1) * 512, e * C:(e + 1) * C].rearrange("(p t) j -> p t j", t=4))
             return raw
 
-        def load_w1(e, b, q):
+        def load_w1(e, q):
             c0, cw = CHUNKS[q]
-            raw = ring.tile([P, 4, cw], F32, name="w1raw%d" % q)
-            nc.sync.dma_start(out=raw[:], in_=w1[e, b * 512:(b + 1) * 512, c0:c0 + cw].rearrange("(p j) c -> p j c", j=4))
-            return raw
+            raws = []
+            for b in range(HB):
+                raw = ring.tile([P, 4, cw], F32, name="w1raw%d" % q, bufs=2)
+                nc.sync.dma_start(out=raw[:], in_=w1[e, b * 512:(b + 1) * 512, c0:c0 + cw].rearrange("(p j) c -> p j c", j=4))
+                raws.append(raw)
+            return raws
 
         def gather(e):
             g4 = ring.tile([P, 4, C], F32, name="g4")
@@ -96,20 +100,23 @@ def tile_moe_bdx_mlp_relu_kernel(tc, dyT, a, w2, w1, gate, offs, out):
                 interleave(eng, grouped[:, s * w:(s + 1) * w, :], g4[:, :, s * w:(s + 1) * w])
             return quantize(grouped[:].rearrange("p c t -> p (c t)"), C, E5, "g%d" % e)
 
+        def group_w2(dst, raw, eng):
+            copy_on(eng, dst.rearrange("p (t m j) -> p m j t", t=4, j=4), raw[:].rearrange("p j (m t) -> p m j t", t=4))
+
         def make_w2(e, b, raw, eng):
             grouped = ring.tile([P, 2048], BF16, name="w2grp", align_bytes=64)
-            src = raw[:]
-            if eng == "g":
-                copy_on(eng, grouped[:].rearrange("p (t m j) -> p t m j", t=4, j=4), src.rearrange("p j (m t) -> p t m j", t=4))
-            else:
-                copy_on(eng, grouped[:].rearrange("p (t m j) -> p m j t", t=4, j=4), src.rearrange("p j (m t) -> p m j t", t=4))
-            return quantize(grouped[:], 512, E4, "w2_%d%d" % (e, b))
+            group_w2(grouped[:], raw, eng)
+            codes, scales = quantize(grouped[:], 512, E4, "w2_%d%d" % (e, b))
+            return codes[:], scales[:]
 
-        def make_w1(e, b, q, raw, eng):
+        def make_w1(e, q, raws, engs):
             cw = CHUNKS[q][1]
-            grouped = ring.tile([P, cw, 4], BF16, name="w1grp%d" % q, align_bytes=64)
-            interleave(eng, grouped[:], raw[:])
-            return quantize(grouped[:].rearrange("p c t -> p (c t)"), cw, E4, "w1_%d%d%d" % (e, b, q))
+            grouped = ring.tile([P, HB * cw, 4], BF16, name="w1grp%d" % q, align_bytes=64)
+            for b in range(HB):
+                w = cw // len(engs[b])
+                for s, eng in enumerate(engs[b]):
+                    interleave(eng, grouped[:, b * cw + s * w:b * cw + s * w + w, :], raws[b][:, :, s * w:s * w + w])
+            return quantize(grouped[:].rearrange("p c t -> p (c t)"), HB * cw, E4, "w1_%d%d" % (e, q))
 
         def dh_tile(w2q, gq, t):
             bank = psum.tile([P, C], F32, name="dh")
@@ -118,33 +125,39 @@ def tile_moe_bdx_mlp_relu_kernel(tc, dyT, a, w2, w1, gate, offs, out):
                                 rhs=gq[0][:].bitcast(E5), rhs_scale=gq[1][:], start=True, stop=True)
             return bank
 
-        def da_vector(e, b, w2q, gq, raw, eng):
+        def da_vector(e, b, w2q, gq, raw, engs):
             plain = ring.tile([P, 4, C], BF16, name="daplain", align_bytes=64)
             for t in range(4):
                 bank = dh_tile(w2q, gq, t)
                 nc.vector.scalar_tensor_tensor(out=plain[:, t, :], in0=raw[:, t, :], scalar=0.0, in1=bank[:], op0=IS_GT, op1=MULT)
             grouped = ring.tile([P, C, 4], BF16, name="dagrp", align_bytes=64)
-            for s in range(2):
-                interleave(eng, grouped[:, s * 256:(s + 1) * 256, :], plain[:, :, s * 256:(s + 1) * 256])
-            return quantize(grouped[:].rearrange("p c t -> p (c t)"), C, E5, "da_%d%d" % (e, b))
+            w = C // len(engs)
+            for s, eng in enumerate(engs):
+                interleave(eng, grouped[:, s * w:(s + 1) * w, :], plain[:, :, s * w:(s + 1) * w])
+            codes, scales = quantize(grouped[:].rearrange("p c t -> p (c t)"), C, E5, "da_%d%d" % (e, b))
+            return codes[:], scales[:]
 
         def make_mask(raw):
-            mask = ring.tile([P, C, 4], BF16, name="mask", align_bytes=64)
+            mask = keep.tile([P, C, 4], BF16, name="mask", align_bytes=64)
             for s in range(2):
-                nc.gpsimd.tensor_scalar(out=mask[:, s * 256:(s + 1) * 256, :], in0=raw[:, :, s * 256:(s + 1) * 256].rearrange("p t c -> p c t"),
-                                        scalar1=0.0, scalar2=1.0, op0=IS_GT, op1=MULT)
+                h = slice(s * 256, (s + 1) * 256)
+                sign = ring.tile([P, 256, 4], BF16, name="sign", align_bytes=64)
+                nc.scalar.activation(out=sign[:].rearrange("p (c i) t -> p c t i", i=4),
+                                     in_=raw[:, :, h].rearrange("p t (c i) -> p c t i", i=4), func=ACT.Sign)
+                nc.scalar.activation(out=mask[:, h, :], in_=sign[:], func=ACT.Relu)
             return mask
 
-        def da_gpsimd(e, b, w2q, gq, mask):
+        def da_split(e, b, w2q, gq, mask):
             plain = ring.tile([P, 4, C], BF16, name="daplain", align_bytes=64)
             for t in range(4):
                 bank = dh_tile(w2q, gq, t)
                 nc.scalar.copy(out=plain[:, t, :], in_=bank[:])
             grouped = ring.tile([P, C, 4], BF16, name="dagrp", align_bytes=64)
-            for s in range(2):
-                nc.gpsimd.tensor_tensor(grouped[:, s * 256:(s + 1) * 256, :], plain[:, :, s * 256:(s + 1) * 256].rearrange("p t c -> p c t"),
-                                        mask[:, s * 256:(s + 1) * 256, :], MULT)
-            return quantize(grouped[:].rearrange("p c t -> p (c t)"), C, E5, "da_%d%d" % (e, b))
+            for s in range(4):
+                h = slice(s * 128, (s + 1) * 128)
+                nc.gpsimd.tensor_tensor(grouped[:, h, :], plain[:, :, h].rearrange("p t c -> p c t"), mask[:, h, :], MULT)
+            codes, scales = quantize(grouped[:].rearrange("p c t -> p (c t)"), C, E5, "da_%d%d" % (e, b))
+            return codes[:], scales[:]
 
         windows = []
         for kt in range(KT):
@@ -153,13 +166,13 @@ def tile_moe_bdx_mlp_relu_kernel(tc, dyT, a, w2, w1, gate, offs, out):
 
         def dx_tile(kt, w1q, daq):
             q = 0 if kt < 2 else 1
-            c0 = kt * P - CHUNKS[q][0]
-            cols = slice(c0, c0 + P)
+            codes, scales = w1q[q]
             bank = psum.tile([P, C], F32, name="dx")
             for b in range(HB):
-                codes, scales = w1q[b, q]
+                c0 = kt * P - CHUNKS[q][0] + b * CHUNKS[q][1]
+                cols = slice(c0, c0 + P)
                 nc.tensor.matmul_mx(out=bank[:], lhsT=codes[:, cols].bitcast(E4), lhsT_scale=scales[:, cols],
-                                    rhs=daq[b][0][:].bitcast(E5), rhs_scale=daq[b][1][:], start=(b == 0), stop=(b == HB - 1))
+                                    rhs=daq[b][0].bitcast(E5), rhs_scale=daq[b][1], start=(b == 0), stop=(b == HB - 1))
             staged = ring.tile([P, C], F32, name="staged", bufs=6)
             nc.scalar.copy(out=staged[:], in_=bank[:])
             return staged
@@ -171,37 +184,31 @@ def tile_moe_bdx_mlp_relu_kernel(tc, dyT, a, w2, w1, gate, offs, out):
         load_gate(0)
         for t in range(1, 4):
             load_dy(t)
-        w2raw = [load_w2(0, b) for b in range(HB)]
         load_gate(1)
-        araw = [load_a(0, b) for b in range(HB)]
-        w1raw = {}
-        for q in range(2):
-            for b in range(HB):
-                w1raw[b, q] = load_w1(0, b, q)
+        w2raw = [load_w2(0, b) for b in range(HB)]
+        a00 = load_a(0, 0)
+        w1raw_a = load_w1(0, 0)
+        a01 = load_a(0, 1)
+        w1raw_b = load_w1(0, 1)
 
-        g4 = gather(0)
-        gq = make_g(0, g4, "vs")
-        w2q = [make_w2(0, 0, w2raw[0], "v"), make_w2(0, 1, w2raw[1], "s")]
-        daq = [da_vector(0, b, w2q[b], gq, araw[b], "s") for b in range(HB)]
-        w1q = {}
-        for q, engs in ((0, "ss"), (1, "ss")):
-            for b in range(HB):
-                w1q[b, q] = make_w1(0, b, q, w1raw[b, q], engs[b])
+        gq = make_g(0, gather(0), "vs")
+        w2q = [make_w2(0, b, w2raw[b], "s") for b in range(HB)]
+        g41 = gather(1)
+        daq = [da_vector(0, 0, w2q[0], gq, a00, "ss"), da_vector(0, 1, w2q[1], gq, a01, "s")]
+        w1q = [make_w1(0, 0, w1raw_a, ("s", "s")), make_w1(0, 1, w1raw_b, ("g", "v"))]
+
+        a11 = load_a(1, 1)
+        w2raw1 = load_w2(1, 1)
+        w1raw_a = load_w1(1, 0)
+        a10 = load_a(1, 0)
+        w2raw0 = load_w2(1, 0)
+        w1raw_b = load_w1(1, 1)
+
+        gq = make_g(1, g41, "g")
+        w2q = [make_w2(1, 0, w2raw0, "g"), make_w2(1, 1, w2raw1, "g")]
         staged0 = [dx_tile(kt, w1q, daq) for kt in range(KT)]
-
-        g4 = gather(1)
-        gq = make_g(1, g4, "s")
-        w2raw = [load_w2(1, b) for b in range(HB)]
-        araw = [load_a(1, b) for b in range(HB)]
-        for q in range(2):
-            for b in range(HB):
-                w1raw[b, q] = load_w1(1, b, q)
-        w2q = [make_w2(1, 0, w2raw[0], "s"), make_w2(1, 1, w2raw[1], "s")]
-        daq = [da_vector(1, b, w2q[b], gq, araw[b], "s") for b in range(HB)]
-        w1q = {}
-        for q, engs in ((0, "ss"), (1, "gg")):
-            for b in range(HB):
-                w1q[b, q] = make_w1(1, b, q, w1raw[b, q], engs[b])
+        w1q = [make_w1(1, 0, w1raw_a, ("s", "g")), make_w1(1, 1, w1raw_b, ("ss", "gg"))]
+        daq = [da_split(1, 0, w2q[0], gq, make_mask(a10)), da_vector(1, 1, w2q[1], gq, a11, "s")]
         for kt in range(KT):
             scatter(0, kt, staged0[kt])
         for kt in range(KT):

@@ -22,7 +22,6 @@ ACT = mybir.ActivationFunctionType
 P = 128
 HB = H // 512
 KT = K // P
-CHUNKS = ((0, 256), (256, 512))
 
 
 def tile_moe_bdx_mlp_relu_kernel(tc, dyT, a, w2, w1, gate, offs, out):
@@ -68,9 +67,9 @@ def tile_moe_bdx_mlp_relu_kernel(tc, dyT, a, w2, w1, gate, offs, out):
             nc.sync.dma_start(out=g[:], in_=gate[0:P, e * C:(e + 1) * C])
             gates.append(g)
 
-        def load_w2(e, b):
-            raw = ring.tile([P, 4, 512], F32, name="w2raw")
-            nc.sync.dma_start(out=raw[:], in_=w2[e, :, b * 512:(b + 1) * 512].rearrange("(p j) c -> p j c", j=4))
+        def load_w2(e):
+            raw = ring.tile([P, 4, H], F32, name="w2raw", bufs=1)
+            nc.sync.dma_start(out=raw[:], in_=w2[e].rearrange("(p j) c -> p j c", j=4))
             return raw
 
         def load_a(e, b):
@@ -78,14 +77,10 @@ def tile_moe_bdx_mlp_relu_kernel(tc, dyT, a, w2, w1, gate, offs, out):
             nc.sync.dma_start(out=raw[:], in_=a[b * 512:(b + 1) * 512, e * C:(e + 1) * C].rearrange("(p t) j -> p t j", t=4))
             return raw
 
-        def load_w1(e, q):
-            c0, cw = CHUNKS[q]
-            raws = []
-            for b in range(HB):
-                raw = ring.tile([P, 4, cw], F32, name="w1raw%d" % q, bufs=2)
-                nc.sync.dma_start(out=raw[:], in_=w1[e, b * 512:(b + 1) * 512, c0:c0 + cw].rearrange("(p j) c -> p j c", j=4))
-                raws.append(raw)
-            return raws
+        def load_w1(e, b):
+            raw = ring.tile([P, 4, K], F32, name="w1raw")
+            nc.sync.dma_start(out=raw[:], in_=w1[e, b * 512:(b + 1) * 512, :].rearrange("(p j) c -> p j c", j=4))
+            return raw
 
         def gather(e):
             g4 = ring.tile([P, 4, C], F32, name="g4")
@@ -100,23 +95,28 @@ def tile_moe_bdx_mlp_relu_kernel(tc, dyT, a, w2, w1, gate, offs, out):
                 interleave(eng, grouped[:, s * w:(s + 1) * w, :], g4[:, :, s * w:(s + 1) * w])
             return quantize(grouped[:].rearrange("p c t -> p (c t)"), C, E5, "g%d" % e)
 
-        def group_w2(dst, raw, eng):
-            copy_on(eng, dst.rearrange("p (t m j) -> p m j t", t=4, j=4), raw[:].rearrange("p j (m t) -> p m j t", t=4))
-
         def make_w2(e, b, raw, eng):
             grouped = ring.tile([P, 2048], BF16, name="w2grp", align_bytes=64)
-            group_w2(grouped[:], raw, eng)
+            src = raw[:, :, b * 512:(b + 1) * 512]
+            if eng == "g":
+                copy_on(eng, grouped[:].rearrange("p (t m j) -> p t m j", t=4, j=4), src.rearrange("p j (m t) -> p t m j", t=4))
+            else:
+                copy_on(eng, grouped[:].rearrange("p (t m j) -> p m j t", t=4, j=4), src.rearrange("p j (m t) -> p m j t", t=4))
             codes, scales = quantize(grouped[:], 512, E4, "w2_%d%d" % (e, b))
             return codes[:], scales[:]
 
-        def make_w1(e, q, raws, engs):
-            cw = CHUNKS[q][1]
-            grouped = ring.tile([P, HB * cw, 4], BF16, name="w1grp%d" % q, align_bytes=64)
+        def make_w1(e, raws, engs):
+            grouped = ring.tile([P, HB * K, 4], BF16, name="w1grp", align_bytes=64, bufs=1)
             for b in range(HB):
-                w = cw // len(engs[b])
+                w = K // len(engs[b])
                 for s, eng in enumerate(engs[b]):
-                    interleave(eng, grouped[:, b * cw + s * w:b * cw + s * w + w, :], raws[b][:, :, s * w:s * w + w])
-            return quantize(grouped[:].rearrange("p c t -> p (c t)"), HB * cw, E4, "w1_%d%d" % (e, q))
+                    interleave(eng, grouped[:, b * K + s * w:b * K + s * w + w, :], raws[b][:, :, s * w:s * w + w])
+            codes = keep.tile([P, HB * K], U32, name="w1_%d_codes" % e, align_bytes=64)
+            scales = keep.tile([P, HB * K], U8, name="w1_%d_scales" % e, align_bytes=64)
+            flat = grouped[:].rearrange("p c t -> p (c t)")
+            for c0, c1 in ((0, 1024), (1024, 1536)):
+                nc.vector.quantize_mx(out=codes[:, c0:c1].bitcast(E4), scales=scales[:, c0:c1], in_=flat[:, 4 * c0:4 * c1])
+            return codes, scales
 
         def dh_tile(w2q, gq, t):
             bank = psum.tile([P, C], F32, name="dh")
@@ -138,13 +138,10 @@ def tile_moe_bdx_mlp_relu_kernel(tc, dyT, a, w2, w1, gate, offs, out):
             return codes[:], scales[:]
 
         def make_mask(raw):
-            mask = keep.tile([P, C, 4], BF16, name="mask", align_bytes=64)
-            for s in range(2):
-                h = slice(s * 256, (s + 1) * 256)
-                sign = ring.tile([P, 256, 4], BF16, name="sign", align_bytes=64)
-                nc.scalar.activation(out=sign[:].rearrange("p (c i) t -> p c t i", i=4),
-                                     in_=raw[:, :, h].rearrange("p t (c i) -> p c t i", i=4), func=ACT.Sign)
-                nc.scalar.activation(out=mask[:, h, :], in_=sign[:], func=ACT.Relu)
+            sign = ring.tile([P, C, 4], BF16, name="sign", align_bytes=64, bufs=1)
+            nc.scalar.activation(out=sign[:].rearrange("p (c i) t -> p c t i", i=4), in_=raw[:].rearrange("p t (c i) -> p c t i", i=4), func=ACT.Sign)
+            mask = ring.tile([P, C, 4], BF16, name="mask", align_bytes=64, bufs=1)
+            nc.scalar.activation(out=mask[:], in_=sign[:], func=ACT.Relu)
             return mask
 
         def da_split(e, b, w2q, gq, mask):
@@ -165,12 +162,10 @@ def tile_moe_bdx_mlp_relu_kernel(tc, dyT, a, w2, w1, gate, offs, out):
             windows.append(window)
 
         def dx_tile(kt, w1q, daq):
-            q = 0 if kt < 2 else 1
-            codes, scales = w1q[q]
+            codes, scales = w1q
             bank = psum.tile([P, C], F32, name="dx")
             for b in range(HB):
-                c0 = kt * P - CHUNKS[q][0] + b * CHUNKS[q][1]
-                cols = slice(c0, c0 + P)
+                cols = slice(b * K + kt * P, b * K + kt * P + P)
                 nc.tensor.matmul_mx(out=bank[:], lhsT=codes[:, cols].bitcast(E4), lhsT_scale=scales[:, cols],
                                     rhs=daq[b][0].bitcast(E5), rhs_scale=daq[b][1], start=(b == 0), stop=(b == HB - 1))
             staged = ring.tile([P, C], F32, name="staged", bufs=6)
@@ -185,33 +180,33 @@ def tile_moe_bdx_mlp_relu_kernel(tc, dyT, a, w2, w1, gate, offs, out):
         for t in range(1, 4):
             load_dy(t)
         load_gate(1)
-        w2raw = [load_w2(0, b) for b in range(HB)]
+        w2raw = load_w2(0)
         a00 = load_a(0, 0)
-        w1raw_a = load_w1(0, 0)
         a01 = load_a(0, 1)
-        w1raw_b = load_w1(0, 1)
+        w1raw0 = load_w1(0, 0)
+        w1raw1 = load_w1(0, 1)
 
-        gq = make_g(0, gather(0), "vs")
-        w2q = [make_w2(0, b, w2raw[b], "s") for b in range(HB)]
-        g41 = gather(1)
-        daq = [da_vector(0, 0, w2q[0], gq, a00, "ss"), da_vector(0, 1, w2q[1], gq, a01, "s")]
-        w1q = [make_w1(0, 0, w1raw_a, ("s", "s")), make_w1(0, 1, w1raw_b, ("g", "v"))]
+        gq = make_g(0, gather(0), "s")
+        w2q0, w2q1 = make_w2(0, 0, w2raw, "v"), make_w2(0, 1, w2raw, "s")
+        w1q = make_w1(0, (w1raw0, w1raw1), ("s", "s"))
+        daq = (da_vector(0, 0, w2q0, gq, a00, "g"), da_vector(0, 1, w2q1, gq, a01, "v"))
 
-        a11 = load_a(1, 1)
-        w2raw1 = load_w2(1, 1)
-        w1raw_a = load_w1(1, 0)
+        w2raw = load_w2(1)
         a10 = load_a(1, 0)
-        w2raw0 = load_w2(1, 0)
-        w1raw_b = load_w1(1, 1)
+        a11 = load_a(1, 1)
+        w1raw0 = load_w1(1, 0)
+        w1raw1 = load_w1(1, 1)
 
-        gq = make_g(1, g41, "g")
-        w2q = [make_w2(1, 0, w2raw0, "g"), make_w2(1, 1, w2raw1, "g")]
-        staged0 = [dx_tile(kt, w1q, daq) for kt in range(KT)]
-        w1q = [make_w1(1, 0, w1raw_a, ("s", "g")), make_w1(1, 1, w1raw_b, ("ss", "gg"))]
-        daq = [da_split(1, 0, w2q[0], gq, make_mask(a10)), da_vector(1, 1, w2q[1], gq, a11, "s")]
+        gq1 = make_g(1, gather(1), "gs")
+        scatter(0, 0, dx_tile(0, w1q, daq))
+        w2q0, w2q1 = make_w2(1, 0, w2raw, "s"), make_w2(1, 1, w2raw, "s")
+        for kt in (1, 2, 3):
+            scatter(0, kt, dx_tile(kt, w1q, daq))
+        da0 = da_split(1, 0, w2q0, gq1, make_mask(a10))
+        scatter(0, 4, dx_tile(4, w1q, daq))
+        w1q1 = make_w1(1, (w1raw0, w1raw1), ("s", "s"))
+        da1 = da_vector(1, 1, w2q1, gq1, a11, "s")
+        scatter(0, 5, dx_tile(5, w1q, daq))
         for kt in range(KT):
-            scatter(0, kt, staged0[kt])
-        for kt in range(KT):
-            staged = dx_tile(kt, w1q, daq)
-            scatter(1, kt, staged)
+            scatter(1, kt, dx_tile(kt, w1q1, (da0, da1)))
             nc.sync.dma_start(out=out[kt * P:(kt + 1) * P, :], in_=windows[kt][:])

from contextlib import ExitStack

import concourse.mybir as mybir

E, C, T = 2, 512, 1024
K, H, N = 768, 1024, 512
FLOPS = 2 * E * C * (N * H + H * K)
BYTES = 4 * (N * T + H * E * C + E * N * H + E * H * K + E * C + K * T) + 2 * 128 * (E * C // 16)

F32 = mybir.dt.float32
BF16 = mybir.dt.bfloat16
U32 = mybir.dt.uint32
U16 = mybir.dt.uint16
U8 = mybir.dt.uint8
E4 = mybir.dt.float8_e4m3fn_x4
E5 = mybir.dt.float8_e5m2_x4
MULT = mybir.AluOpType.mult
ADD = mybir.AluOpType.add
IS_GT = mybir.AluOpType.is_gt
ACT = mybir.ActivationFunctionType

P = 128
HB = H // 512
KT = K // P


def tile_moe_bdx_mlp_relu_kernel(tc, dyT, a, w2, w1, gate, offs, out):
    nc = tc.nc
    with ExitStack() as ctx:
        keep = ctx.enter_context(tc.tile_pool(name="keep", bufs=1))
        ring = ctx.enter_context(tc.tile_pool(name="ring", bufs=2))
        psum = ctx.enter_context(tc.psum_pool(name="psum", bufs=4))

        def copy_on(eng, out_ap, in_ap):
            if eng == "v":
                nc.vector.tensor_copy(out=out_ap, in_=in_ap)
            elif eng == "s":
                nc.scalar.copy(out=out_ap, in_=in_ap)
            else:
                nc.gpsimd.tensor_scalar(out=out_ap, in0=in_ap, scalar1=1.0, scalar2=0.0, op0=MULT, op1=ADD)

        def interleave(eng, dst, src):
            if eng == "g":
                copy_on(eng, dst.rearrange("p c t -> p c t"), src.rearrange("p t c -> p c t"))
            else:
                copy_on(eng, dst.rearrange("p (c i) t -> p c t i", i=4), src.rearrange("p t (c i) -> p c t i", i=4))

        def quantize(src, width, fmt, name):
            codes = keep.tile([P, width], U32, name=name + "_codes", align_bytes=64)
            scales = keep.tile([P, width], U8, name=name + "_scales", align_bytes=64)
            nc.vector.quantize_mx(out=codes[:].bitcast(fmt), scales=scales[:], in_=src)
            return codes, scales

        offs_t = keep.tile([P, E * C // 16], U16, name="offs_t")
        nc.sync.dma_start(offs_t[:], offs)
        dy_view = dyT.rearrange("(p t) j -> p t j", t=4)
        dy = []
        gates = []

        def load_dy(t):
            plane = keep.tile([P, T], F32, name="dy%d" % t)
            nc.sync.dma_start(out=plane[:], in_=dy_view[:, t, :])
            dy.append(plane)

        def load_gate(e):
            g = keep.tile([P, C], F32, name="gate%d" % e)
            nc.sync.dma_start(out=g[:], in_=gate[0:P, e * C:(e + 1) * C])
            gates.append(g)

        def load_w2(e):
            raw = ring.tile([P, 4, H], F32, name="w2raw", bufs=1)
            nc.sync.dma_start(out=raw[:], in_=w2[e].rearrange("(p j) c -> p j c", j=4))
            return raw

        def load_a(e, b):
            raw = ring.tile([P, 4, C], F32, name="araw")
            nc.sync.dma_start(out=raw[:], in_=a[b * 512:(b + 1) * 512, e * C:(e + 1) * C].rearrange("(p t) j -> p t j", t=4))
            return raw

        def load_w1(e, b):
            raw = ring.tile([P, 4, K], F32, name="w1raw")
            nc.sync.dma_start(out=raw[:], in_=w1[e, b * 512:(b + 1) * 512, :].rearrange("(p j) c -> p j c", j=4))
            return raw

        def gather(e):
            g4 = ring.tile([P, 4, C], F32, name="g4")
            for t in range(4):
                nc.vector.tensor_tensor(g4[:, t, :], dy[t][:].indirect(offs_t[:, e * (C // 16):(e + 1) * (C // 16)]), gates[e][:], MULT)
            return g4

        def make_g(e, g4, engs):
            grouped = ring.tile([P, C, 4], BF16, name="ggrp", align_bytes=64)
            w = C // len(engs)
            for s, eng in enumerate(engs):
                interleave(eng, grouped[:, s * w:(s + 1) * w, :], g4[:, :, s * w:(s + 1) * w])
            return quantize(grouped[:].rearrange("p c t -> p (c t)"), C, E5, "g%d" % e)

        def make_w2(e, b, raw, eng):
            grouped = ring.tile([P, 2048], BF16, name="w2grp", align_bytes=64)
            src = raw[:, :, b * 512:(b + 1) * 512]
            if eng == "g":
                copy_on(eng, grouped[:].rearrange("p (t m j) -> p t m j", t=4, j=4), src.rearrange("p j (m t) -> p t m j", t=4))
            else:
                copy_on(eng, grouped[:].rearrange("p (t m j) -> p m j t", t=4, j=4), src.rearrange("p j (m t) -> p m j t", t=4))
            codes, scales = quantize(grouped[:], 512, E4, "w2_%d%d" % (e, b))
            return codes[:], scales[:]

        def make_w1(e, raws, engs):
            grouped = ring.tile([P, HB * K, 4], BF16, name="w1grp", align_bytes=64, bufs=1)
            for b in range(HB):
                w = K // len(engs[b])
                for s, eng in enumerate(engs[b]):
                    interleave(eng, grouped[:, b * K + s * w:b * K + s * w + w, :], raws[b][:, :, s * w:s * w + w])
            codes = keep.tile([P, HB * K], U32, name="w1_%d_codes" % e, align_bytes=64)
            scales = keep.tile([P, HB * K], U8, name="w1_%d_scales" % e, align_bytes=64)
            flat = grouped[:].rearrange("p c t -> p (c t)")
            for c0, c1 in ((0, 1024), (1024, 1536)):
                nc.vector.quantize_mx(out=codes[:, c0:c1].bitcast(E4), scales=scales[:, c0:c1], in_=flat[:, 4 * c0:4 * c1])
            return codes, scales

        def dh_tile(w2q, gq, t):
            bank = psum.tile([P, C], F32, name="dh")
            cols = slice(t * P, (t + 1) * P)
            nc.tensor.matmul_mx(out=bank[:], lhsT=w2q[0][:, cols].bitcast(E4), lhsT_scale=w2q[1][:, cols],
                                rhs=gq[0][:].bitcast(E5), rhs_scale=gq[1][:], start=True, stop=True)
            return bank

        def da_vector(e, b, w2q, gq, raw, engs):
            plain = ring.tile([P, 4, C], BF16, name="daplain", align_bytes=64)
            for t in range(4):
                bank = dh_tile(w2q, gq, t)
                nc.vector.scalar_tensor_tensor(out=plain[:, t, :], in0=raw[:, t, :], scalar=0.0, in1=bank[:], op0=IS_GT, op1=MULT)
            grouped = ring.tile([P, C, 4], BF16, name="dagrp", align_bytes=64)
            w = C // len(engs)
            for s, eng in enumerate(engs):
                interleave(eng, grouped[:, s * w:(s + 1) * w, :], plain[:, :, s * w:(s + 1) * w])
            codes, scales = quantize(grouped[:].rearrange("p c t -> p (c t)"), C, E5, "da_%d%d" % (e, b))
            return codes[:], scales[:]

        def make_mask(raw):
            sign = ring.tile([P, C, 4], BF16, name="sign", align_bytes=64, bufs=1)
            nc.scalar.activation(out=sign[:].rearrange("p (c i) t -> p c t i", i=4), in_=raw[:].rearrange("p t (c i) -> p c t i", i=4), func=ACT.Sign)
            mask = ring.tile([P, C, 4], BF16, name="mask", align_bytes=64, bufs=1)
            nc.scalar.activation(out=mask[:], in_=sign[:], func=ACT.Relu)
            return mask

        def da_split(e, b, w2q, gq, mask):
            plain = ring.tile([P, 4, C], BF16, name="daplain", align_bytes=64)
            for t in range(4):
                bank = dh_tile(w2q, gq, t)
                nc.scalar.copy(out=plain[:, t, :], in_=bank[:])
            grouped = ring.tile([P, C, 4], BF16, name="dagrp", align_bytes=64)
            for s in range(4):
                h = slice(s * 128, (s + 1) * 128)
                nc.gpsimd.tensor_tensor(grouped[:, h, :], plain[:, :, h].rearrange("p t c -> p c t"), mask[:, h, :], MULT)
            codes, scales = quantize(grouped[:].rearrange("p c t -> p (c t)"), C, E5, "da_%d%d" % (e, b))
            return codes[:], scales[:]

        windows = []
        for kt in range(KT):
            window = keep.tile([P, T], F32, name="window%d" % kt)
            windows.append(window)

        def dx_tile(kt, w1q, daq):
            codes, scales = w1q
            bank = psum.tile([P, C], F32, name="dx")
            for b in range(HB):
                cols = slice(b * K + kt * P, b * K + kt * P + P)
                nc.tensor.matmul_mx(out=bank[:], lhsT=codes[:, cols].bitcast(E4), lhsT_scale=scales[:, cols],
                                    rhs=daq[b][0].bitcast(E5), rhs_scale=daq[b][1], start=(b == 0), stop=(b == HB - 1))
            staged = ring.tile([P, C], F32, name="staged", bufs=6)
            nc.scalar.copy(out=staged[:], in_=bank[:])
            return staged

        def scatter(e, kt, staged):
            nc.vector.tensor_copy(out=windows[kt][:].indirect(offs_t[:, e * (C // 16):(e + 1) * (C // 16)]), in_=staged[:])

        load_dy(0)
        load_gate(0)
        for t in range(1, 4):
            load_dy(t)
        load_gate(1)
        w2raw = load_w2(0)
        a00 = load_a(0, 0)
        a01 = load_a(0, 1)
        w1raw0 = load_w1(0, 0)
        w1raw1 = load_w1(0, 1)

        gq = make_g(0, gather(0), "s")
        w2q0, w2q1 = make_w2(0, 0, w2raw, "v"), make_w2(0, 1, w2raw, "s")
        w1q = make_w1(0, (w1raw0, w1raw1), ("s", "s"))
        daq = (da_vector(0, 0, w2q0, gq, a00, "g"), da_vector(0, 1, w2q1, gq, a01, "v"))

        w2raw = load_w2(1)
        a10 = load_a(1, 0)
        a11 = load_a(1, 1)
        w1raw0 = load_w1(1, 0)
        w1raw1 = load_w1(1, 1)

        gq1 = make_g(1, gather(1), "gs")
        scatter(0, 0, dx_tile(0, w1q, daq))
        w2q0, w2q1 = make_w2(1, 0, w2raw, "s"), make_w2(1, 1, w2raw, "s")
        for kt in (1, 2, 3):
            scatter(0, kt, dx_tile(kt, w1q, daq))
        da0 = da_split(1, 0, w2q0, gq1, make_mask(a10))
        scatter(0, 4, dx_tile(4, w1q, daq))
        w1q1 = make_w1(1, (w1raw0, w1raw1), ("s", "s"))
        da1 = da_vector(1, 1, w2q1, gq1, a11, "s")
        scatter(0, 5, dx_tile(5, w1q, daq))
        for kt in range(KT):
            scatter(1, kt, dx_tile(kt, w1q1, (da0, da1)))
            nc.sync.dma_start(out=out[kt * P:(kt + 1) * P, :], in_=windows[kt][:])
